import numpy as np
import ml_dtypes


def mxq(x, axis, fmt="e4m3"):
    dtype, down = {"e4m3": (ml_dtypes.float8_e4m3fn, 7), "e5m2": (ml_dtypes.float8_e5m2, 14)}[fmt]
    v = np.moveaxis(np.asarray(x, np.float32).astype(ml_dtypes.bfloat16).astype(np.float64), axis, -1)
    blocks = v.reshape(v.shape[:-1] + (-1, 32))
    amax = np.abs(blocks).max(-1, keepdims=True)
    byte = np.maximum(np.where(amax > 0, np.frexp(amax)[1] - 1 + 127, 0) - down, 1)
    scale = np.exp2(byte - 127.0)
    codes = (blocks / scale).astype(np.float32).astype(dtype).astype(np.float64)
    return np.moveaxis((codes * scale).reshape(v.shape), -1, axis)


WIDE = False


def mx_kscale(k):
    if not WIDE:
        return np.ones(k)
    levels = np.array([30, -30])
    if k % 512:
        return np.exp2(np.random.permutation(np.resize(levels, k // 32))).repeat(32)
    a = np.empty((k // 512, 16))
    for p in range(k // 512):
        a[p, :8] = np.random.permutation(np.resize(levels, 8))
        for g in range(8):
            far = levels[np.abs(levels - a[p, g]) >= 10]
            a[p, g + 8] = far[np.random.randint(len(far))]
    return np.exp2(a.ravel()).repeat(32)


def f64(x):
    return np.asarray(x).astype(np.float64)


def striped(idx):
    return np.tile(np.asarray(idx).reshape(-1, 16).T, (8, 1)).astype(np.uint16)


def unstriped(offs):
    return offs[:16].T.reshape(-1).astype(np.int64)


E2M1 = np.array([0.0, 0.5, 1.0, 1.5, 2.0, 3.0, 4.0, 6.0, -0.0, -0.5, -1.0, -1.5, -2.0, -3.0, -4.0, -6.0])


def pack_weight(w, fmt):
    k, n = w.shape
    w = f64(np.asarray(w, np.float32).astype(ml_dtypes.bfloat16)).reshape(k // 32, 32, n)
    amax = np.abs(w).max(1)
    if fmt == "e4m3":
        byte = np.frexp(amax)[1] - 1 + 127 - 7
    else:
        mant, ex = np.frexp(amax / 6.0)
        byte = np.where(mant > 0.5, ex, ex - 1) + 127
    byte = np.clip(np.where(amax > 0, byte, 1), 1, 254)
    scaled = (w * np.exp2(127.0 - byte)[:, None, :]).reshape(k, n).astype(np.float32)
    by_word = np.ascontiguousarray(scaled.reshape(k // 512, 128, 4, n).transpose(0, 1, 3, 2))
    if fmt == "e4m3":
        words = by_word.astype(ml_dtypes.float8_e4m3fn).view(np.uint8)
    else:
        c = by_word.astype(ml_dtypes.float4_e2m1fn).view(np.uint8) & 0xF
        words = (c[..., 0::2] | (c[..., 1::2] << 4)).reshape(k // 512, 128, 2 * n)
    return np.ascontiguousarray(words), np.ascontiguousarray(byte.astype(np.uint8).reshape(k // 512, 16, n))


def unpack_weight(words, scales, fmt):
    g, _, n = scales.shape
    words = np.ascontiguousarray(words).reshape(g, 128, n, -1)
    if fmt == "e4m3":
        vals = words.view(ml_dtypes.float8_e4m3fn).astype(np.float64)
    else:
        nib = np.empty((g, 128, n, 4), np.uint8)
        nib[..., 0::2] = words & 0xF
        nib[..., 1::2] = words >> 4
        vals = E2M1[nib]
    vals = vals * np.repeat(np.exp2(scales.astype(np.float64) - 127.0), 8, axis=1)[..., None]
    return vals.transpose(0, 1, 3, 2).reshape(g * 512, n)


K, T, J, I, L, S, R, C, O, N = 1024, 1024, 256, 128, 128, 512, 512, 1024, 256, 256


def setup_inputs():
    n = np.random.standard_normal
    idx = np.random.permutation(T)[:I]
    idx2 = np.random.permutation(S)[:L]
    idx3 = np.random.permutation(C)[:J]
    idx4 = np.random.permutation(C)[:O]
    fk = mx_kscale(K)
    fr = mx_kscale(R)
    wp = pack_weight(n((K, R)) * 1 / np.sqrt(K) * fk[:, None] * fr, "e2m1")
    wbp = pack_weight(n((R, N)) * 1 / np.sqrt(R) / fr[:, None], "e4m3")
    return {
        "xa": (n((K, T)) / fk[:, None]).astype(np.float32),
        "xb": (n((K, S)) * 0.6 / fk[:, None]).astype(np.float32),
        "w_words": wp[0],
        "w_scales": wp[1],
        "oldh": (n((R, C)) * 0.7 * fr[:, None]).astype(np.float32),
        "wb_words": wbp[0],
        "wb_scales": wbp[1],
        "rs": (1.0 * n((O, N))).astype(np.float32),
        "offs": striped(idx),
        "offs2": striped(idx2),
        "offs3": striped(idx3),
        "offs4": striped(idx4),
    }


def reference(xa, xb, w_words, w_scales, oldh, wb_words, wb_scales, rs, offs, offs2, offs3, offs4):
    idx = unstriped(offs)
    idx2 = unstriped(offs2)
    idx3 = unstriped(offs3)
    idx4 = unstriped(offs4)
    wu = unpack_weight(w_words, w_scales, "e2m1")
    wbu = unpack_weight(wb_words, wb_scales, "e4m3")
    u = np.concatenate([f64(xa)[:, idx], f64(xb)[:, idx2]], axis=1)
    uq = mxq(u, 0, "e4m3")
    a = wu.T @ uq
    ha = np.maximum(a, 0.0)
    pw0 = np.zeros((R, C))
    pw0[:, idx3] = ha
    pg = pw0 + f64(oldh)
    hid = pg[:, idx4]
    hidq = mxq(hid, 0, "e5m2")
    p = hidq.T @ wbu
    mn = np.mean(np.abs(p), axis=1, keepdims=True)
    y = np.maximum(p - mn, 0.0) - 0.3 * f64(rs)
    return y

@@ -1,0 +1,184 @@
+from contextlib import ExitStack
+
+import concourse.mybir as mybir
+
+K, T, J, S, R, C, O, N = 1024, 1024, 256, 512, 512, 1024, 256, 256
+FLOPS = 2 * K * R * J + 2 * R * O * N
+
+F32 = mybir.dt.float32
+BF16 = mybir.dt.bfloat16
+I32 = mybir.dt.int32
+U32 = mybir.dt.uint32
+U16 = mybir.dt.uint16
+U8 = mybir.dt.uint8
+E4M3 = mybir.dt.float8_e4m3fn_x4
+E5M2 = mybir.dt.float8_e5m2_x4
+E2M1 = mybir.dt.float4_e2m1fn_x4
+ALU = mybir.AluOpType
+ACT = mybir.ActivationFunctionType
+
+P = 128
+PACK = 4
+PASSES = K // (P * PACK)
+HALF = 128
+LIST_COLS = HALF // 16
+
+
+def tile_list_page_joined_rowabove_kernel(
+    tc, xa, xb, w_words, w_scales, oldh, wb_words, wb_scales, rs, offs, offs2, offs3, offs4, out
+):
+    nc = tc.nc
+    with ExitStack() as ctx:
+        lists = ctx.enter_context(tc.tile_pool(name="lists", bufs=1))
+        sb = ctx.enter_context(tc.tile_pool(name="sb", bufs=1))
+        psum = ctx.enter_context(tc.psum_pool(name="psum", bufs=1))
+
+        idx_a = lists.tile([P, LIST_COLS], U16, name="idx_a")
+        idx_b = lists.tile([P, LIST_COLS], U16, name="idx_b")
+        idx_put = lists.tile([P, 2 * LIST_COLS], U16, name="idx_put")
+        idx_read = lists.tile([P, 2 * LIST_COLS], U16, name="idx_read")
+
+        ws_raw = sb.tile([P, PASSES, R], U8, name="ws_raw", align_bytes=64)
+        wbs = sb.tile([P, N], U8, name="wbs", align_bytes=64)
+        nc.vector.memset(ws_raw[:].rearrange("p z c -> p (z c)").bitcast(I32), 0)
+        nc.gpsimd.memset(wbs[:].bitcast(I32), 0)
+        for q in range(4):
+            nc.scalar.dma_start(
+                ws_raw[32 * q : 32 * q + 4, :, :].bitcast(I32),
+                w_scales[:, 4 * q : 4 * q + 4, :].rearrange("z r c -> r z c").bitcast(I32),
+            )
+        for q in range(4):
+            nc.gpsimd.dma_start(
+                wbs[32 * q : 32 * q + 4, :].bitcast(I32),
+                wb_scales[0, 4 * q : 4 * q + 4, :].bitcast(I32),
+            )
+
+        def load_planes(name, src, z, first, count):
+            width = src.shape[1]
+            tile = sb.tile([P, count, width], F32, name=name)
+            rows = src[512 * z : 512 * (z + 1), :].rearrange("(p i) c -> p i c", i=PACK)
+            nc.sync.dma_start(tile[:], rows[:, first : first + count, :])
+            return [tile[:, i, :] for i in range(count)]
+
+        xb_planes = [load_planes("xb0", xb, 0, 0, 4)]
+        nc.sync.dma_start(idx_b[:], offs2)
+        w_raw = sb.tile([P, PASSES, 2 * R], U8, name="w_raw", align_bytes=64)
+        nc.sync.dma_start(w_raw[:].bitcast(I32), w_words.rearrange("z p c -> p z c").bitcast(I32))
+        xb_planes.append(load_planes("xb1", xb, 1, 0, 4))
+        nc.sync.dma_start(idx_a[:], offs)
+        xa_planes = [load_planes("xa0a", xa, 0, 0, 2) + load_planes("xa0b", xa, 0, 2, 2)]
+        nc.sync.dma_start(idx_put[:], offs3)
+        xa_planes.append(
+            load_planes("xa1a", xa, 1, 0, 2) + load_planes("xa1b", xa, 1, 2, 1) + load_planes("xa1c", xa, 1, 3, 1)
+        )
+        old = [load_planes("old%d" % t, oldh, 0, t, 1)[0] for t in range(PACK)]
+        nc.sync.dma_start(idx_read[:], offs4)
+        wb = sb.tile([P, N], U32, name="wb", align_bytes=64)
+        nc.sync.dma_start(wb[:].bitcast(I32), wb_words[0].rearrange("p c r -> p (c r)").bitcast(I32))
+        res = sb.tile([P, 2, N], F32, name="res")
+        nc.sync.dma_start(res[:], rs.rearrange("(h p) n -> p h n", p=P))
+
+        placed = [sb.tile([P, C], F32, name="placed%d" % t) for t in range(PACK)]
+        for t in range(PACK):
+            nc.vector.memset(placed[t][:], 0.0)
+
+        w_dealt = sb.tile([P, PASSES, PACK, 2 * P], U8, name="w_dealt", align_bytes=64)
+        ws_dealt = sb.tile([P, PASSES, PACK, P], U8, name="ws_dealt", align_bytes=64)
+
+        def deal(z):
+            nc.vector.tensor_copy(
+                w_dealt[:, z, :, :].rearrange("p t (q b) -> p t q b", b=2),
+                w_raw[:, z, :].rearrange("p (q t b) -> p t q b", t=PACK, b=2),
+            )
+            nc.vector.tensor_copy(
+                ws_dealt[:, z, :, :],
+                ws_raw[:, z, :].rearrange("p (q t) -> p t q", t=PACK),
+            )
+
+        def gather_quantise(name, planes, idx):
+            u = sb.tile([P, HALF, PACK], BF16, name="u_" + name, align_bytes=64)
+            for i in range(PACK):
+                nc.vector.tensor_copy(u[:, :, i], planes[i].indirect(idx[:]))
+            codes = sb.tile([P, HALF], U32, name="uc_" + name, align_bytes=64)
+            scales = sb.tile([P, HALF], U8, name="us_" + name, align_bytes=64)
+            nc.vector.quantize_mx(codes[:].bitcast(E4M3), scales[:], u[:].rearrange("p j i -> p (j i)"))
+            return codes, scales
+
+        def first_product(acc, t, z, uq):
+            nc.tensor.matmul_mx(
+                acc,
+                lhsT=w_dealt[:, z, t, :].bitcast(E2M1),
+                lhsT_scale=ws_dealt[:, z, t, :],
+                rhs=uq[0][:].bitcast(E4M3),
+                rhs_scale=uq[1][:],
+                start=(z == 0),
+                stop=(z == PASSES - 1),
+            )
+
+        ub = []
+        for z in range(PASSES):
+            ub.append(gather_quantise("b%d" % z, xb_planes[z], idx_b))
+            deal(z)
+        acc_b = psum.tile([P, PACK, HALF], F32, name="acc_b")
+        for t in range(PACK):
+            for z in range(PASSES):
+                first_product(acc_b[:, t, :], t, z, ub[z])
+        ha_b = sb.tile([P, PACK, HALF], F32, name="ha_b")
+        nc.scalar.activation(ha_b[:], acc_b[:], ACT.Relu)
+        for t in range(PACK):
+            nc.scalar.activation(placed[t][:].indirect(idx_put[:, LIST_COLS:]), ha_b[:, t, :], ACT.Copy)
+
+        acc_a = [psum.tile([P, HALF], F32, name="acc_a%d" % t) for t in range(PACK)]
+        for z in range(PASSES):
+            ua = gather_quantise("a%d" % z, xa_planes[z], idx_a)
+            for t in range(PACK):
+                first_product(acc_a[t][:], t, z, ua)
+        for t in range(PACK):
+            ha_a = sb.tile([P, HALF], F32, name="ha_a%d" % t)
+            window = placed[t][:].indirect(idx_put[:, :LIST_COLS])
+            if t == 1:
+                nc.vector.tensor_scalar(ha_a[:], acc_a[t][:], 0.0, None, ALU.max)
+                nc.vector.tensor_copy(window, ha_a[:])
+            else:
+                nc.scalar.activation(ha_a[:], acc_a[t][:], ACT.Relu)
+                nc.scalar.activation(window, ha_a[:], ACT.Copy)
+
+        hid = sb.tile([P, PACK, O], BF16, name="hid")
+        for t in range(PACK):
+            page = sb.tile([P, C], F32, name="page%d" % t)
+            nc.vector.tensor_tensor(page[:], placed[t][:], old[t], ALU.add)
+            if t < PACK - 1:
+                nc.scalar.activation(hid[:, t, :], page[:].indirect(idx_read[:]), ACT.Copy)
+            else:
+                nc.vector.tensor_copy(hid[:, t, :HALF], page[:].indirect(idx_read[:, :LIST_COLS]))
+                nc.scalar.activation(hid[:, t, HALF:], page[:].indirect(idx_read[:, LIST_COLS:]), ACT.Copy)
+
+        for h in range(2):
+            woven = sb.tile([P, HALF, PACK], BF16, name="woven%d" % h, align_bytes=64)
+            src = hid[:, :, h * HALF : (h + 1) * HALF].rearrange("p t (c i) -> p c t i", i=4)
+            dst = woven[:].rearrange("p (c i) t -> p c t i", i=4)
+            if h == 0:
+                nc.vector.tensor_copy(dst, src)
+            else:
+                nc.scalar.copy(dst, src)
+            codes = sb.tile([P, HALF], U32, name="hc%d" % h, align_bytes=64)
+            scales = sb.tile([P, HALF], U8, name="hs%d" % h, align_bytes=64)
+            nc.vector.quantize_mx(codes[:].bitcast(E5M2), scales[:], woven[:].rearrange("p o t -> p (o t)"))
+            acc = psum.tile([P, N], F32, name="acc_p%d" % h)
+            nc.tensor.matmul_mx(
+                acc[:],
+                lhsT=codes[:].bitcast(E5M2),
+                lhsT_scale=scales[:],
+                rhs=wb[:].bitcast(E4M3),
+                rhs_scale=wbs[:],
+                start=True,
+                stop=True,
+            )
+            mag = sb.tile([P, N], F32, name="mag%d" % h)
+            mean = sb.tile([P, 1], F32, name="mean%d" % h)
+            nc.scalar.activation(mag[:], acc[:], ACT.Abs, scale=1.0 / N, accum_out=mean[:])
+            off = sb.tile([P, N], F32, name="off%d" % h)
+            nc.vector.tensor_scalar(off[:], res[:, h, :], 0.3, mean[:], ALU.mult, ALU.add)
+            y = sb.tile([P, N], F32, name="y%d" % h)
+            nc.vector.scalar_tensor_tensor(y[:], acc[:], mean[:], off[:], ALU.max, ALU.subtract)
+            nc.sync.dma_start(out[h * HALF : (h + 1) * HALF, :], y[:])

@@ -41,6 +41,9 @@ def tile_list_page_joined_rowabove_kernel(
         ws_raw = sb.tile([P, PASSES, R], U8, name="ws_raw", align_bytes=64)
         wbs = sb.tile([P, N], U8, name="wbs", align_bytes=64)
         nc.vector.memset(ws_raw[:].rearrange("p z c -> p (z c)").bitcast(I32), 0)
+        placed = [sb.tile([P, C], F32, name="placed%d" % t) for t in range(PACK)]
+        for t in range(PACK):
+            nc.gpsimd.memset(placed[t][:], 0.0)
         nc.gpsimd.memset(wbs[:].bitcast(I32), 0)
         for q in range(4):
             nc.scalar.dma_start(
@@ -55,40 +58,36 @@ def tile_list_page_joined_rowabove_kernel(
 
         def load_planes(name, src, z, first, count):
             width = src.shape[1]
-            tile = sb.tile([P, count, width], F32, name=name)
+            tile = sb.tile([P, count, width], F32, name=name, align_bytes=64)
             rows = src[512 * z : 512 * (z + 1), :].rearrange("(p i) c -> p i c", i=PACK)
             nc.sync.dma_start(tile[:], rows[:, first : first + count, :])
             return [tile[:, i, :] for i in range(count)]
 
-        xb_planes = [load_planes("xb0", xb, 0, 0, 4)]
-        nc.sync.dma_start(idx_b[:], offs2)
         w_raw = sb.tile([P, PASSES, 2 * R], U8, name="w_raw", align_bytes=64)
         nc.sync.dma_start(w_raw[:].bitcast(I32), w_words.rearrange("z p c -> p z c").bitcast(I32))
+        xb_planes = [load_planes("xb0", xb, 0, 0, 4)]
+        nc.sync.dma_start(idx_b[:], offs2)
         xb_planes.append(load_planes("xb1", xb, 1, 0, 4))
         nc.sync.dma_start(idx_a[:], offs)
-        xa_planes = [load_planes("xa0a", xa, 0, 0, 2) + load_planes("xa0b", xa, 0, 2, 2)]
+        xa_planes = [load_planes("xa0", xa, 0, 0, 4)]
         nc.sync.dma_start(idx_put[:], offs3)
         xa_planes.append(
             load_planes("xa1a", xa, 1, 0, 2) + load_planes("xa1b", xa, 1, 2, 1) + load_planes("xa1c", xa, 1, 3, 1)
         )
-        old = [load_planes("old%d" % t, oldh, 0, t, 1)[0] for t in range(PACK)]
+        old = load_planes("old01", oldh, 0, 0, 2) + load_planes("old23", oldh, 0, 2, 2)
         nc.sync.dma_start(idx_read[:], offs4)
         wb = sb.tile([P, N], U32, name="wb", align_bytes=64)
         nc.sync.dma_start(wb[:].bitcast(I32), wb_words[0].rearrange("p c r -> p (c r)").bitcast(I32))
         res = sb.tile([P, 2, N], F32, name="res")
         nc.sync.dma_start(res[:], rs.rearrange("(h p) n -> p h n", p=P))
 
-        placed = [sb.tile([P, C], F32, name="placed%d" % t) for t in range(PACK)]
-        for t in range(PACK):
-            nc.vector.memset(placed[t][:], 0.0)
-
         w_dealt = sb.tile([P, PASSES, PACK, 2 * P], U8, name="w_dealt", align_bytes=64)
         ws_dealt = sb.tile([P, PASSES, PACK, P], U8, name="ws_dealt", align_bytes=64)
 
         def deal(z):
             nc.vector.tensor_copy(
-                w_dealt[:, z, :, :].rearrange("p t (q b) -> p t q b", b=2),
-                w_raw[:, z, :].rearrange("p (q t b) -> p t q b", t=PACK, b=2),
+                w_dealt[:, z, :, :].bitcast(U16),
+                w_raw[:, z, :].bitcast(U16).rearrange("p (q t) -> p t q", t=PACK),
             )
             nc.vector.tensor_copy(
                 ws_dealt[:, z, :, :],
@@ -115,10 +114,9 @@ def tile_list_page_joined_rowabove_kernel(
                 stop=(z == PASSES - 1),
             )
 
-        ub = []
         for z in range(PASSES):
-            ub.append(gather_quantise("b%d" % z, xb_planes[z], idx_b))
             deal(z)
+        ub = [gather_quantise("b%d" % z, xb_planes[z], idx_b) for z in range(PASSES)]
         acc_b = psum.tile([P, PACK, HALF], F32, name="acc_b")
         for t in range(PACK):
             for z in range(PASSES):
@@ -133,37 +131,40 @@ def tile_list_page_joined_rowabove_kernel(
             ua = gather_quantise("a%d" % z, xa_planes[z], idx_a)
             for t in range(PACK):
                 first_product(acc_a[t][:], t, z, ua)
+        ha_a = [sb.tile([P, HALF], F32, name="ha_a%d" % t) for t in range(PACK)]
+        nc.scalar.activation(ha_a[0][:], acc_a[0][:], ACT.Relu)
+        for t in range(1, PACK):
+            nc.vector.tensor_scalar(ha_a[t][:], acc_a[t][:], 0.0, None, ALU.max)
         for t in range(PACK):
-            ha_a = sb.tile([P, HALF], F32, name="ha_a%d" % t)
             window = placed[t][:].indirect(idx_put[:, :LIST_COLS])
             if t == 1:
-                nc.vector.tensor_scalar(ha_a[:], acc_a[t][:], 0.0, None, ALU.max)
-                nc.vector.tensor_copy(window, ha_a[:])
+                nc.vector.tensor_copy(window, ha_a[t][:])
             else:
-                nc.scalar.activation(ha_a[:], acc_a[t][:], ACT.Relu)
-                nc.scalar.activation(window, ha_a[:], ACT.Copy)
+                nc.scalar.activation(window, ha_a[t][:], ACT.Copy)
 
-        hid = sb.tile([P, PACK, O], BF16, name="hid")
+        hid = sb.tile([P, PACK - 1, O], BF16, name="hid")
+        pages = []
         for t in range(PACK):
             page = sb.tile([P, C], F32, name="page%d" % t)
             nc.vector.tensor_tensor(page[:], placed[t][:], old[t], ALU.add)
+            pages.append(page)
             if t < PACK - 1:
                 nc.scalar.activation(hid[:, t, :], page[:].indirect(idx_read[:]), ACT.Copy)
-            else:
-                nc.vector.tensor_copy(hid[:, t, :HALF], page[:].indirect(idx_read[:, :LIST_COLS]))
-                nc.scalar.activation(hid[:, t, HALF:], page[:].indirect(idx_read[:, LIST_COLS:]), ACT.Copy)
+        woven = [sb.tile([P, HALF, PACK], BF16, name="woven%d" % h, align_bytes=64) for h in range(2)]
+        for h in range(2):
+            nc.vector.tensor_copy(
+                woven[h][:, :, : PACK - 1],
+                hid[:, :, h * HALF : (h + 1) * HALF].rearrange("p t o -> p o t"),
+            )
+            nc.vector.tensor_copy(
+                woven[h][:, :, PACK - 1],
+                pages[PACK - 1][:].indirect(idx_read[:, h * LIST_COLS : (h + 1) * LIST_COLS]),
+            )
 
         for h in range(2):
-            woven = sb.tile([P, HALF, PACK], BF16, name="woven%d" % h, align_bytes=64)
-            src = hid[:, :, h * HALF : (h + 1) * HALF].rearrange("p t (c i) -> p c t i", i=4)
-            dst = woven[:].rearrange("p (c i) t -> p c t i", i=4)
-            if h == 0:
-                nc.vector.tensor_copy(dst, src)
-            else:
-                nc.scalar.copy(dst, src)
             codes = sb.tile([P, HALF], U32, name="hc%d" % h, align_bytes=64)
             scales = sb.tile([P, HALF], U8, name="hs%d" % h, align_bytes=64)
-            nc.vector.quantize_mx(codes[:].bitcast(E5M2), scales[:], woven[:].rearrange("p o t -> p (o t)"))
+            nc.vector.quantize_mx(codes[:].bitcast(E5M2), scales[:], woven[h][:].rearrange("p o t -> p (o t)"))
             acc = psum.tile([P, N], F32, name="acc_p%d" % h)
             nc.tensor.matmul_mx(
                 acc[:],

@@ -40,21 +40,8 @@ def tile_list_page_joined_rowabove_kernel(
 
         ws_raw = sb.tile([P, PASSES, R], U8, name="ws_raw", align_bytes=64)
         wbs = sb.tile([P, N], U8, name="wbs", align_bytes=64)
-        nc.vector.memset(ws_raw[:].rearrange("p z c -> p (z c)").bitcast(I32), 0)
-        placed = [sb.tile([P, C], F32, name="placed%d" % t) for t in range(PACK)]
-        for t in range(PACK):
-            nc.gpsimd.memset(placed[t][:], 0.0)
+        nc.gpsimd.memset(ws_raw[:].rearrange("p z c -> p (z c)").bitcast(I32), 0)
         nc.gpsimd.memset(wbs[:].bitcast(I32), 0)
-        for q in range(4):
-            nc.scalar.dma_start(
-                ws_raw[32 * q : 32 * q + 4, :, :].bitcast(I32),
-                w_scales[:, 4 * q : 4 * q + 4, :].rearrange("z r c -> r z c").bitcast(I32),
-            )
-        for q in range(4):
-            nc.gpsimd.dma_start(
-                wbs[32 * q : 32 * q + 4, :].bitcast(I32),
-                wb_scales[0, 4 * q : 4 * q + 4, :].bitcast(I32),
-            )
 
         def load_planes(name, src, z, first, count):
             width = src.shape[1]
@@ -63,23 +50,37 @@ def tile_list_page_joined_rowabove_kernel(
             nc.sync.dma_start(tile[:], rows[:, first : first + count, :])
             return [tile[:, i, :] for i in range(count)]
 
+        xb_planes = [load_planes("xb0", xb, 0, 0, 4)]
+        for q in range(4):
+            nc.sync.dma_start(
+                ws_raw[32 * q : 32 * q + 4, :, :].bitcast(I32),
+                w_scales[:, 4 * q : 4 * q + 4, :].rearrange("z r c -> r z c").bitcast(I32),
+            )
         w_raw = sb.tile([P, PASSES, 2 * R], U8, name="w_raw", align_bytes=64)
         nc.sync.dma_start(w_raw[:].bitcast(I32), w_words.rearrange("z p c -> p z c").bitcast(I32))
-        xb_planes = [load_planes("xb0", xb, 0, 0, 4)]
         nc.sync.dma_start(idx_b[:], offs2)
         xb_planes.append(load_planes("xb1", xb, 1, 0, 4))
         nc.sync.dma_start(idx_a[:], offs)
         xa_planes = [load_planes("xa0", xa, 0, 0, 4)]
         nc.sync.dma_start(idx_put[:], offs3)
+        nc.sync.dma_start(idx_read[:], offs4)
         xa_planes.append(
             load_planes("xa1a", xa, 1, 0, 2) + load_planes("xa1b", xa, 1, 2, 1) + load_planes("xa1c", xa, 1, 3, 1)
         )
-        old = load_planes("old01", oldh, 0, 0, 2) + load_planes("old23", oldh, 0, 2, 2)
-        nc.sync.dma_start(idx_read[:], offs4)
+        old = [load_planes("old%d" % t, oldh, 0, t, 1)[0] for t in range(PACK)]
         wb = sb.tile([P, N], U32, name="wb", align_bytes=64)
         nc.sync.dma_start(wb[:].bitcast(I32), wb_words[0].rearrange("p c r -> p (c r)").bitcast(I32))
+        for q in range(4):
+            nc.sync.dma_start(
+                wbs[32 * q : 32 * q + 4, :].bitcast(I32),
+                wb_scales[0, 4 * q : 4 * q + 4, :].bitcast(I32),
+            )
         res = sb.tile([P, 2, N], F32, name="res")
         nc.sync.dma_start(res[:], rs.rearrange("(h p) n -> p h n", p=P))
+
+        placed = [sb.tile([P, C], F32, name="placed%d" % t) for t in range(PACK)]
+        for t in range(PACK):
+            nc.vector.memset(placed[t][:], 0.0)
 
         w_dealt = sb.tile([P, PASSES, PACK, 2 * P], U8, name="w_dealt", align_bytes=64)
         ws_dealt = sb.tile([P, PASSES, PACK, P], U8, name="ws_dealt", align_bytes=64)
@@ -117,14 +118,14 @@ def tile_list_page_joined_rowabove_kernel(
         for z in range(PASSES):
             deal(z)
         ub = [gather_quantise("b%d" % z, xb_planes[z], idx_b) for z in range(PASSES)]
-        acc_b = psum.tile([P, PACK, HALF], F32, name="acc_b")
+        acc_b = [psum.tile([P, HALF], F32, name="acc_b%d" % t, tag="bank%d" % t) for t in range(PACK)]
+        for z in range(PASSES):
+            for t in range(PACK):
+                first_product(acc_b[t][:], t, z, ub[z])
         for t in range(PACK):
-            for z in range(PASSES):
-                first_product(acc_b[:, t, :], t, z, ub[z])
-        ha_b = sb.tile([P, PACK, HALF], F32, name="ha_b")
-        nc.scalar.activation(ha_b[:], acc_b[:], ACT.Relu)
-        for t in range(PACK):
-            nc.scalar.activation(placed[t][:].indirect(idx_put[:, LIST_COLS:]), ha_b[:, t, :], ACT.Copy)
+            ha_b = sb.tile([P, HALF], F32, name="ha_b%d" % t)
+            nc.scalar.activation(ha_b[:], acc_b[t][:], ACT.Relu)
+            nc.scalar.activation(placed[t][:].indirect(idx_put[:, LIST_COLS:]), ha_b[:], ACT.Copy)
 
         acc_a = [psum.tile([P, HALF], F32, name="acc_a%d" % t) for t in range(PACK)]
         for z in range(PASSES):
@@ -132,40 +133,39 @@ def tile_list_page_joined_rowabove_kernel(
             for t in range(PACK):
                 first_product(acc_a[t][:], t, z, ua)
         ha_a = [sb.tile([P, HALF], F32, name="ha_a%d" % t) for t in range(PACK)]
+        windows = [placed[t][:].indirect(idx_put[:, :LIST_COLS]) for t in range(PACK)]
         nc.scalar.activation(ha_a[0][:], acc_a[0][:], ACT.Relu)
-        for t in range(1, PACK):
+        nc.scalar.activation(windows[0], ha_a[0][:], ACT.Copy)
+        for t in (1, 2):
             nc.vector.tensor_scalar(ha_a[t][:], acc_a[t][:], 0.0, None, ALU.max)
-        for t in range(PACK):
-            window = placed[t][:].indirect(idx_put[:, :LIST_COLS])
-            if t == 1:
-                nc.vector.tensor_copy(window, ha_a[t][:])
-            else:
-                nc.scalar.activation(window, ha_a[t][:], ACT.Copy)
+        nc.vector.tensor_copy(windows[1], ha_a[1][:])
+        nc.scalar.activation(windows[2], ha_a[2][:], ACT.Copy)
+        nc.scalar.activation(ha_a[3][:], acc_a[3][:], ACT.Relu)
+        nc.scalar.activation(windows[3], ha_a[3][:], ACT.Copy)
 
-        hid = sb.tile([P, PACK - 1, O], BF16, name="hid")
-        pages = []
+        hid = sb.tile([P, PACK, O], BF16, name="hid")
         for t in range(PACK):
             page = sb.tile([P, C], F32, name="page%d" % t)
             nc.vector.tensor_tensor(page[:], placed[t][:], old[t], ALU.add)
-            pages.append(page)
             if t < PACK - 1:
                 nc.scalar.activation(hid[:, t, :], page[:].indirect(idx_read[:]), ACT.Copy)
+            else:
+                nc.vector.tensor_copy(hid[:, t, :HALF], page[:].indirect(idx_read[:, :LIST_COLS]))
+                nc.scalar.activation(hid[:, t, HALF:], page[:].indirect(idx_read[:, LIST_COLS:]), ACT.Copy)
         woven = [sb.tile([P, HALF, PACK], BF16, name="woven%d" % h, align_bytes=64) for h in range(2)]
         for h in range(2):
-            nc.vector.tensor_copy(
-                woven[h][:, :, : PACK - 1],
-                hid[:, :, h * HALF : (h + 1) * HALF].rearrange("p t o -> p o t"),
-            )
-            nc.vector.tensor_copy(
-                woven[h][:, :, PACK - 1],
-                pages[PACK - 1][:].indirect(idx_read[:, h * LIST_COLS : (h + 1) * LIST_COLS]),
+            weave = nc.vector.tensor_copy if h == 0 else nc.scalar.copy
+            weave(
+                woven[h][:].rearrange("p (c i) t -> p c t i", i=4),
+                hid[:, :, h * HALF : (h + 1) * HALF].rearrange("p t (c i) -> p c t i", i=4),
             )
 
+        rows = []
         for h in range(2):
             codes = sb.tile([P, HALF], U32, name="hc%d" % h, align_bytes=64)
             scales = sb.tile([P, HALF], U8, name="hs%d" % h, align_bytes=64)
             nc.vector.quantize_mx(codes[:].bitcast(E5M2), scales[:], woven[h][:].rearrange("p o t -> p (o t)"))
-            acc = psum.tile([P, N], F32, name="acc_p%d" % h)
+            acc = psum.tile([P, N], F32, name="acc_p%d" % h, tag="bank%d" % h)
             nc.tensor.matmul_mx(
                 acc[:],
                 lhsT=codes[:].bitcast(E5M2),
@@ -180,6 +180,8 @@ def tile_list_page_joined_rowabove_kernel(
             nc.scalar.activation(mag[:], acc[:], ACT.Abs, scale=1.0 / N, accum_out=mean[:])
             off = sb.tile([P, N], F32, name="off%d" % h)
             nc.vector.tensor_scalar(off[:], res[:, h, :], 0.3, mean[:], ALU.mult, ALU.add)
+            rows.append((acc, mean, off))
+        for h, (acc, mean, off) in enumerate(rows):
             y = sb.tile([P, N], F32, name="y%d" % h)
             nc.vector.scalar_tensor_tensor(y[:], acc[:], mean[:], off[:], ALU.max, ALU.subtract)
             nc.sync.dma_start(out[h * HALF : (h + 1) * HALF, :], y[:])

@@ -63,11 +63,11 @@ def tile_list_page_joined_rowabove_kernel(
         nc.sync.dma_start(idx_a[:], offs)
         xa_planes = [load_planes("xa0", xa, 0, 0, 4)]
         nc.sync.dma_start(idx_put[:], offs3)
-        nc.sync.dma_start(idx_read[:], offs4)
         xa_planes.append(
             load_planes("xa1a", xa, 1, 0, 2) + load_planes("xa1b", xa, 1, 2, 1) + load_planes("xa1c", xa, 1, 3, 1)
         )
-        old = [load_planes("old%d" % t, oldh, 0, t, 1)[0] for t in range(PACK)]
+        nc.sync.dma_start(idx_read[:], offs4)
+        old = load_planes("old0", oldh, 0, 0, 1) + load_planes("old1", oldh, 0, 1, 1) + load_planes("old23", oldh, 0, 2, 2)
         wb = sb.tile([P, N], U32, name="wb", align_bytes=64)
         nc.sync.dma_start(wb[:].bitcast(I32), wb_words[0].rearrange("p c r -> p (c r)").bitcast(I32))
         for q in range(4):
@@ -143,21 +143,23 @@ def tile_list_page_joined_rowabove_kernel(
         nc.scalar.activation(ha_a[3][:], acc_a[3][:], ACT.Relu)
         nc.scalar.activation(windows[3], ha_a[3][:], ACT.Copy)
 
-        hid = sb.tile([P, PACK, O], BF16, name="hid")
+        hid = sb.tile([P, PACK - 1, O], BF16, name="hid")
+        pages = []
         for t in range(PACK):
             page = sb.tile([P, C], F32, name="page%d" % t)
             nc.vector.tensor_tensor(page[:], placed[t][:], old[t], ALU.add)
+            pages.append(page)
             if t < PACK - 1:
                 nc.scalar.activation(hid[:, t, :], page[:].indirect(idx_read[:]), ACT.Copy)
-            else:
-                nc.vector.tensor_copy(hid[:, t, :HALF], page[:].indirect(idx_read[:, :LIST_COLS]))
-                nc.scalar.activation(hid[:, t, HALF:], page[:].indirect(idx_read[:, LIST_COLS:]), ACT.Copy)
         woven = [sb.tile([P, HALF, PACK], BF16, name="woven%d" % h, align_bytes=64) for h in range(2)]
         for h in range(2):
-            weave = nc.vector.tensor_copy if h == 0 else nc.scalar.copy
-            weave(
-                woven[h][:].rearrange("p (c i) t -> p c t i", i=4),
-                hid[:, :, h * HALF : (h + 1) * HALF].rearrange("p t (c i) -> p c t i", i=4),
+            nc.vector.tensor_copy(
+                woven[h][:, :, : PACK - 1],
+                hid[:, :, h * HALF : (h + 1) * HALF].rearrange("p t o -> p o t"),
+            )
+            nc.vector.tensor_copy(
+                woven[h][:, :, PACK - 1],
+                pages[PACK - 1][:].indirect(idx_read[:, h * LIST_COLS : (h + 1) * LIST_COLS]),
             )
 
         rows = []

from contextlib import ExitStack

import concourse.mybir as mybir

K, T, J, S, R, C, O, N = 1024, 1024, 256, 512, 512, 1024, 256, 256
FLOPS = 2 * K * R * J + 2 * R * O * N

F32 = mybir.dt.float32
BF16 = mybir.dt.bfloat16
I32 = mybir.dt.int32
U32 = mybir.dt.uint32
U16 = mybir.dt.uint16
U8 = mybir.dt.uint8
E4M3 = mybir.dt.float8_e4m3fn_x4
E5M2 = mybir.dt.float8_e5m2_x4
E2M1 = mybir.dt.float4_e2m1fn_x4
ALU = mybir.AluOpType
ACT = mybir.ActivationFunctionType

P = 128
PACK = 4
PASSES = K // (P * PACK)
HALF = 128
LIST_COLS = HALF // 16


def tile_list_page_joined_rowabove_kernel(
    tc, xa, xb, w_words, w_scales, oldh, wb_words, wb_scales, rs, offs, offs2, offs3, offs4, out
):
    nc = tc.nc
    with ExitStack() as ctx:
        lists = ctx.enter_context(tc.tile_pool(name="lists", bufs=1))
        sb = ctx.enter_context(tc.tile_pool(name="sb", bufs=1))
        psum = ctx.enter_context(tc.psum_pool(name="psum", bufs=1))

        idx_a = lists.tile([P, LIST_COLS], U16, name="idx_a")
        idx_b = lists.tile([P, LIST_COLS], U16, name="idx_b")
        idx_put = lists.tile([P, 2 * LIST_COLS], U16, name="idx_put")
        idx_read = lists.tile([P, 2 * LIST_COLS], U16, name="idx_read")

        ws_raw = sb.tile([P, PASSES, R], U8, name="ws_raw", align_bytes=64)
        wbs = sb.tile([P, N], U8, name="wbs", align_bytes=64)
        nc.gpsimd.memset(ws_raw[:].rearrange("p z c -> p (z c)").bitcast(I32), 0)
        nc.gpsimd.memset(wbs[:].bitcast(I32), 0)

        def load_planes(name, src, z, first, count):
            width = src.shape[1]
            tile = sb.tile([P, count, width], F32, name=name, align_bytes=64)
            rows = src[512 * z : 512 * (z + 1), :].rearrange("(p i) c -> p i c", i=PACK)
            nc.sync.dma_start(tile[:], rows[:, first : first + count, :])
            return [tile[:, i, :] for i in range(count)]

        xb_planes = [load_planes("xb0", xb, 0, 0, 4)]
        for q in range(4):
            nc.sync.dma_start(
                ws_raw[32 * q : 32 * q + 4, :, :].bitcast(I32),
                w_scales[:, 4 * q : 4 * q + 4, :].rearrange("z r c -> r z c").bitcast(I32),
            )
        w_raw = sb.tile([P, PASSES, 2 * R], U8, name="w_raw", align_bytes=64)
        nc.sync.dma_start(w_raw[:].bitcast(I32), w_words.rearrange("z p c -> p z c").bitcast(I32))
        nc.sync.dma_start(idx_b[:], offs2)
        xb_planes.append(load_planes("xb1", xb, 1, 0, 4))
        nc.sync.dma_start(idx_a[:], offs)
        xa_planes = [load_planes("xa0", xa, 0, 0, 4)]
        nc.sync.dma_start(idx_put[:], offs3)
        xa_planes.append(
            load_planes("xa1a", xa, 1, 0, 2) + load_planes("xa1b", xa, 1, 2, 1) + load_planes("xa1c", xa, 1, 3, 1)
        )
        nc.sync.dma_start(idx_read[:], offs4)
        old = load_planes("old0", oldh, 0, 0, 1) + load_planes("old1", oldh, 0, 1, 1) + load_planes("old23", oldh, 0, 2, 2)
        wb = sb.tile([P, N], U32, name="wb", align_bytes=64)
        nc.sync.dma_start(wb[:].bitcast(I32), wb_words[0].rearrange("p c r -> p (c r)").bitcast(I32))
        for q in range(4):
            nc.sync.dma_start(
                wbs[32 * q : 32 * q + 4, :].bitcast(I32),
                wb_scales[0, 4 * q : 4 * q + 4, :].bitcast(I32),
            )
        res = sb.tile([P, 2, N], F32, name="res")
        nc.sync.dma_start(res[:], rs.rearrange("(h p) n -> p h n", p=P))

        placed = [sb.tile([P, C], F32, name="placed%d" % t) for t in range(PACK)]
        for t in range(PACK):
            nc.vector.memset(placed[t][:], 0.0)

        w_dealt = sb.tile([P, PASSES, PACK, 2 * P], U8, name="w_dealt", align_bytes=64)
        ws_dealt = sb.tile([P, PASSES, PACK, P], U8, name="ws_dealt", align_bytes=64)

        def deal(z):
            nc.vector.tensor_copy(
                w_dealt[:, z, :, :].bitcast(U16),
                w_raw[:, z, :].bitcast(U16).rearrange("p (q t) -> p t q", t=PACK),
            )
            nc.vector.tensor_copy(
                ws_dealt[:, z, :, :],
                ws_raw[:, z, :].rearrange("p (q t) -> p t q", t=PACK),
            )

        def gather_quantise(name, planes, idx):
            u = sb.tile([P, HALF, PACK], BF16, name="u_" + name, align_bytes=64)
            for i in range(PACK):
                nc.vector.tensor_copy(u[:, :, i], planes[i].indirect(idx[:]))
            codes = sb.tile([P, HALF], U32, name="uc_" + name, align_bytes=64)
            scales = sb.tile([P, HALF], U8, name="us_" + name, align_bytes=64)
            nc.vector.quantize_mx(codes[:].bitcast(E4M3), scales[:], u[:].rearrange("p j i -> p (j i)"))
            return codes, scales

        def first_product(acc, t, z, uq):
            nc.tensor.matmul_mx(
                acc,
                lhsT=w_dealt[:, z, t, :].bitcast(E2M1),
                lhsT_scale=ws_dealt[:, z, t, :],
                rhs=uq[0][:].bitcast(E4M3),
                rhs_scale=uq[1][:],
                start=(z == 0),
                stop=(z == PASSES - 1),
            )

        for z in range(PASSES):
            deal(z)
        ub = [gather_quantise("b%d" % z, xb_planes[z], idx_b) for z in range(PASSES)]
        acc_b = [psum.tile([P, HALF], F32, name="acc_b%d" % t, tag="bank%d" % t) for t in range(PACK)]
        for z in range(PASSES):
            for t in range(PACK):
                first_product(acc_b[t][:], t, z, ub[z])
        for t in range(PACK):
            ha_b = sb.tile([P, HALF], F32, name="ha_b%d" % t)
            nc.scalar.activation(ha_b[:], acc_b[t][:], ACT.Relu)
            nc.scalar.activation(placed[t][:].indirect(idx_put[:, LIST_COLS:]), ha_b[:], ACT.Copy)

        acc_a = [psum.tile([P, HALF], F32, name="acc_a%d" % t) for t in range(PACK)]
        for z in range(PASSES):
            ua = gather_quantise("a%d" % z, xa_planes[z], idx_a)
            for t in range(PACK):
                first_product(acc_a[t][:], t, z, ua)
        ha_a = [sb.tile([P, HALF], F32, name="ha_a%d" % t) for t in range(PACK)]
        windows = [placed[t][:].indirect(idx_put[:, :LIST_COLS]) for t in range(PACK)]
        nc.scalar.activation(ha_a[0][:], acc_a[0][:], ACT.Relu)
        nc.scalar.activation(windows[0], ha_a[0][:], ACT.Copy)
        for t in (1, 2):
            nc.vector.tensor_scalar(ha_a[t][:], acc_a[t][:], 0.0, None, ALU.max)
        nc.vector.tensor_copy(windows[1], ha_a[1][:])
        nc.scalar.activation(windows[2], ha_a[2][:], ACT.Copy)
        nc.scalar.activation(ha_a[3][:], acc_a[3][:], ACT.Relu)
        nc.scalar.activation(windows[3], ha_a[3][:], ACT.Copy)

        hid = sb.tile([P, PACK - 1, O], BF16, name="hid")
        pages = []
        for t in range(PACK):
            page = sb.tile([P, C], F32, name="page%d" % t)
            nc.vector.tensor_tensor(page[:], placed[t][:], old[t], ALU.add)
            pages.append(page)
            if t < PACK - 1:
                nc.scalar.activation(hid[:, t, :], page[:].indirect(idx_read[:]), ACT.Copy)
        woven = [sb.tile([P, HALF, PACK], BF16, name="woven%d" % h, align_bytes=64) for h in range(2)]
        for h in range(2):
            nc.vector.tensor_copy(
                woven[h][:, :, : PACK - 1],
                hid[:, :, h * HALF : (h + 1) * HALF].rearrange("p t o -> p o t"),
            )
            nc.vector.tensor_copy(
                woven[h][:, :, PACK - 1],
                pages[PACK - 1][:].indirect(idx_read[:, h * LIST_COLS : (h + 1) * LIST_COLS]),
            )

        rows = []
        for h in range(2):
            codes = sb.tile([P, HALF], U32, name="hc%d" % h, align_bytes=64)
            scales = sb.tile([P, HALF], U8, name="hs%d" % h, align_bytes=64)
            nc.vector.quantize_mx(codes[:].bitcast(E5M2), scales[:], woven[h][:].rearrange("p o t -> p (o t)"))
            acc = psum.tile([P, N], F32, name="acc_p%d" % h, tag="bank%d" % h)
            nc.tensor.matmul_mx(
                acc[:],
                lhsT=codes[:].bitcast(E5M2),
                lhsT_scale=scales[:],
                rhs=wb[:].bitcast(E4M3),
                rhs_scale=wbs[:],
                start=True,
                stop=True,
            )
            mag = sb.tile([P, N], F32, name="mag%d" % h)
            mean = sb.tile([P, 1], F32, name="mean%d" % h)
            nc.scalar.activation(mag[:], acc[:], ACT.Abs, scale=1.0 / N, accum_out=mean[:])
            off = sb.tile([P, N], F32, name="off%d" % h)
            nc.vector.tensor_scalar(off[:], res[:, h, :], 0.3, mean[:], ALU.mult, ALU.add)
            rows.append((acc, mean, off))
        for h, (acc, mean, off) in enumerate(rows):
            y = sb.tile([P, N], F32, name="y%d" % h)
            nc.vector.scalar_tensor_tensor(y[:], acc[:], mean[:], off[:], ALU.max, ALU.subtract)
            nc.sync.dma_start(out[h * HALF : (h + 1) * HALF, :], y[:])
